import numpy as np
import ml_dtypes


def mxq(x, axis, fmt="e4m3"):
    dtype, down = {"e4m3": (ml_dtypes.float8_e4m3fn, 7), "e5m2": (ml_dtypes.float8_e5m2, 14)}[fmt]
    v = np.moveaxis(np.asarray(x, np.float32).astype(ml_dtypes.bfloat16).astype(np.float64), axis, -1)
    blocks = v.reshape(v.shape[:-1] + (-1, 32))
    amax = np.abs(blocks).max(-1, keepdims=True)
    byte = np.maximum(np.where(amax > 0, np.frexp(amax)[1] - 1 + 127, 0) - down, 1)
    scale = np.exp2(byte - 127.0)
    codes = (blocks / scale).astype(np.float32).astype(dtype).astype(np.float64)
    return np.moveaxis((codes * scale).reshape(v.shape), -1, axis)


WIDE = False


def mx_kscale(k):
    if not WIDE:
        return np.ones(k)
    levels = np.array([10, -10, 5, -5, 0])
    if k % 512:
        return np.exp2(np.random.permutation(np.resize(levels, k // 32))).repeat(32)
    a = np.empty((k // 512, 16))
    for p in range(k // 512):
        a[p, :8] = np.random.permutation(np.resize(levels, 8))
        for g in range(8):
            far = levels[np.abs(levels - a[p, g]) >= 10]
            a[p, g + 8] = far[np.random.randint(len(far))]
    return np.exp2(a.ravel()).repeat(32)


BF16 = ml_dtypes.bfloat16


def bf(x):
    return np.asarray(x, np.float32).astype(BF16)


def f64(x):
    return np.asarray(x).astype(np.float64)


T, D, F, E, R = 4096, 1024, 256, 128, 512


def softmax_last(l):
    m = np.max(l, axis=-1, keepdims=True)
    p = np.exp(l - m)
    return p / np.sum(p, axis=-1, keepdims=True)


def draw0():
    s, t = mx_kscale(D), mx_kscale(R)
    sd, sr = np.sqrt(D), np.sqrt(R)
    return {
        "x": bf(np.random.standard_normal((T, D)) * s),
        "w0": bf(np.random.standard_normal((D, F)) / sd / s[:, None]),
        "wr": bf(np.random.standard_normal((D, E)) / sd / s[:, None]),
        "br": bf(np.random.standard_normal(E) * 0.5),
        "a": bf(np.random.standard_normal((D, R)) / sd / s[:, None] * t),
        "b": bf(np.random.standard_normal((R, F)) * 0.6 / sr / t[:, None]),
    }


def core(x, w0, wr, br, a, b):
    n_tok = x.shape[0]
    n_exp = wr.shape[1]
    rank = a.shape[1]
    per_exp = rank // n_exp
    xq = mxq(f64(x), 1, "e4m3")
    l = (xq @ mxq(f64(wr), 0, "e4m3")) + f64(br)
    g = float(n_exp) * softmax_last(l)
    u = xq @ mxq(f64(a), 0, "e4m3")
    z = u.reshape(n_tok, n_exp, per_exp) * g[:, :, None]
    z = z.reshape(n_tok, rank)
    y = (xq @ mxq(f64(w0), 0, "e4m3")) + (mxq(z, 1, "e4m3") @ mxq(f64(b), 0, "e4m3"))
    return y


def e4m3fn_bytes(y):
    return np.clip(np.asarray(y, np.float64), -448.0, 448.0).astype(np.float32).astype(ml_dtypes.float8_e4m3fn).view(np.uint8)


def e4m3fn_values(b):
    return np.asarray(b, np.uint8).view(ml_dtypes.float8_e4m3fn).astype(np.float64)


def setup_inputs():
    d = draw0()
    x0 = np.asarray(d['x']).astype(np.float64)
    s = (np.max(np.abs(x0), axis=(0,), keepdims=True) / 448.0).astype(np.float32)
    out = {}
    for k, v in d.items():
        if k == 'x':
            out['x_bytes'] = e4m3fn_bytes(x0 / s.astype(np.float64))
            out['x_scale'] = s
        else:
            out[k] = v
    return out


def reference(x_bytes, x_scale, w0, wr, br, a, b):
    return core(e4m3fn_values(x_bytes) * x_scale.astype(np.float64), w0, wr, br, a, b)

@@ -1,0 +1,338 @@
+from contextlib import ExitStack
+
+import concourse.mybir as mybir
+from concourse.masks import make_identity
+
+T, D, F, E, R = 4096, 1024, 256, 128, 512
+P = 128
+STEP = 256
+N_STEPS = T // STEP
+SLABS = STEP // P
+G = D // 512
+FLOPS = 2 * T * D * (F + E + R) + 2 * T * R * F
+
+F32 = mybir.dt.float32
+BF16 = mybir.dt.bfloat16
+U32 = mybir.dt.uint32
+U8 = mybir.dt.uint8
+FP8 = mybir.dt.float8_e4m3fn
+FP8X4 = mybir.dt.float8_e4m3fn_x4
+ACT = mybir.ActivationFunctionType
+ALU = mybir.AluOpType
+AX = mybir.AxisListType
+
+
+def tile_rankwisemoloradenserouter_t_kernel(tc, x_bytes, x_scale, w0, wr, br, a, b, out):
+    nc = tc.nc
+    with ExitStack() as ctx:
+        keep = ctx.enter_context(tc.tile_pool(name="keep", bufs=1))
+        bytes_pool = ctx.enter_context(tc.tile_pool(name="xbytes", bufs=N_STEPS))
+        sb = ctx.enter_context(tc.tile_pool(name="sb", bufs=3))
+        psum = ctx.enter_context(tc.psum_pool(name="psum", bufs=2))
+        ctx.enter_context(tc.manual_schedule())
+
+        xb = {}
+
+        def load_x(n):
+            t = bytes_pool.tile([P, SLABS, D], U8, name="xb")
+            src = x_bytes[n * STEP : (n + 1) * STEP, :].rearrange("(p s) k -> p s k", s=SLABS)
+            nc.sync.dma_start(out=t[:], in_=src)
+            xb[n] = t
+
+        wr_raw = keep.tile([P, G, 4, E], BF16, name="wr_raw")
+        a_raw = keep.tile([P, G, 4, R], BF16, name="a_raw")
+        w0_raw = keep.tile([P, G, 4, F], BF16, name="w0_raw")
+        b_raw = keep.tile([P, 4, F], BF16, name="b_raw")
+        xs = keep.tile([P, G, 4], F32, name="xs")
+        br_col = keep.tile([P, 1], BF16, name="br_col")
+
+        load_x(0)
+        nc.sync.dma_start(out=wr_raw[:], in_=wr.rearrange("(g p j) n -> p g j n", g=G, j=4))
+        nc.sync.dma_start(out=xs[:], in_=x_scale.rearrange("o (g p t) -> p (o g) t", g=G, t=4))
+        with nc.allow_non_contiguous_dma(reason="one bias value to a partition"):
+            nc.sync.dma_start(out=br_col[:], in_=br.rearrange("(p o) -> p o", o=1))
+        load_x(1)
+        for g in range(G):
+            nc.sync.dma_start(out=a_raw[:, g], in_=a[512 * g : 512 * (g + 1), :].rearrange("(p j) n -> p j n", j=4))
+        load_x(2)
+        nc.sync.dma_start(out=w0_raw[:], in_=w0.rearrange("(g p j) n -> p g j n", g=G, j=4))
+        nc.sync.dma_start(out=b_raw[:], in_=b.rearrange("(p j) n -> p j n", j=4))
+        for n in range(3, N_STEPS):
+            load_x(n)
+
+        warm = keep.tile([P, 1], F32, name="warm")
+        nc.vector.memset(warm[:], 0.0)
+        nc.scalar.activation(out=warm[:], in_=warm[:], func=ACT.Exp)
+        ident = keep.tile([P, P], F32, name="ident")
+        make_identity(nc, ident[:])
+
+        wr_g = keep.tile([P, G, E, 4], BF16, align_bytes=64, name="wr_g")
+        a_g = keep.tile([P, G, R, 4], BF16, align_bytes=64, name="a_g")
+        w0_g = keep.tile([P, G, F, 4], BF16, align_bytes=64, name="w0_g")
+        b_g = keep.tile([P, F, 4], BF16, align_bytes=64, name="b_g")
+        wr_c = keep.tile([P, G, E], U32, align_bytes=64, name="wr_c")
+        wr_s = keep.tile([P, G, E], U8, align_bytes=64, name="wr_s")
+        a_c = keep.tile([P, G, R], U32, align_bytes=64, name="a_c")
+        a_s = keep.tile([P, G, R], U8, align_bytes=64, name="a_s")
+        w0_c = keep.tile([P, G, F], U32, align_bytes=64, name="w0_c")
+        w0_s = keep.tile([P, G, F], U8, align_bytes=64, name="w0_s")
+        b_c = keep.tile([P, F], U32, align_bytes=64, name="b_c")
+        b_s = keep.tile([P, F], U8, align_bytes=64, name="b_s")
+
+        def quantize(codes, scales, grouped):
+            nc.vector.quantize_mx(out=codes.bitcast(FP8X4), scales=scales, in_=grouped)
+
+        def gp_interleave(dst, src):
+            nc.gpsimd.tensor_scalar(dst, src, 1.0, 0.0, op0=ALU.mult, op1=ALU.add)
+
+        def a_interleave(g):
+            nc.vector.tensor_copy(
+                out=a_g[:, g].rearrange("p (t m) j -> p t m j", t=4),
+                in_=a_raw[:, g].rearrange("p j (m t) -> p t m j", t=4),
+            )
+
+        xw, xt, xg, xc, xsc = {}, {}, {}, {}, {}
+        sm, lT_sb, negmax, ex, esum, rsum, gn, g_sb = {}, {}, {}, {}, {}, {}, {}, {}
+        ub, zg, zc, zs, yb = {}, {}, {}, {}, {}
+
+        def widen(n, s):
+            if n >= N_STEPS:
+                return
+            if s == 0:
+                xw[n] = sb.tile([P, SLABS, D], BF16, name="xw")
+            nc.scalar.copy(out=xw[n][:, s], in_=xb[n][:, s].bitcast(FP8))
+
+        def x_transpose(n, g):
+            if n >= N_STEPS:
+                return
+            t = psum.tile([P, 2, STEP], F32, name="xt", bufs=3)
+            for s in range(SLABS):
+                words = xw[n][:, s].bitcast(F32)
+                for u in range(2):
+                    nc.tensor.transpose(
+                        t[:, u, P * s : P * (s + 1)], words[:, 256 * g + u : 256 * (g + 1) : 2], ident[:]
+                    )
+            xt[n, g] = t
+
+        def x_scale_mult(n, g):
+            if n >= N_STEPS:
+                return
+            if g == 0:
+                xg[n] = sb.tile([P, G, STEP, 4], BF16, align_bytes=64, name="xg")
+            src = xt[n, g][:].rearrange("p u n -> p (u n)").bitcast(BF16)
+            nc.vector.tensor_tensor(
+                out=xg[n][:, g].rearrange("p n (u e) -> p n u e", u=2),
+                in0=src.rearrange("p (u n e) -> p n u e", u=2, e=2),
+                in1=xs[:, g].rearrange("p (u e) -> p u e", u=2).unsqueeze(1).to_broadcast([P, STEP, 2, 2]),
+                op=ALU.mult,
+            )
+
+        def x_quantize(n):
+            if n >= N_STEPS:
+                return
+            xc[n] = sb.tile([P, G, STEP], U32, align_bytes=64, name="xc", bufs=6)
+            xsc[n] = sb.tile([P, G, STEP], U8, align_bytes=64, name="xsc", bufs=6)
+            quantize(
+                xc[n][:].rearrange("p g n -> p (g n)"),
+                xsc[n][:].rearrange("p g n -> p (g n)"),
+                xg[n][:].rearrange("p g n t -> p (g n t)"),
+            )
+
+        def logits(n):
+            if n >= N_STEPS:
+                return
+            sm[n] = psum.tile([P, 2, STEP], F32, name="sm")
+            for g in range(G):
+                nc.tensor.matmul_mx(
+                    out=sm[n][:, 0],
+                    lhsT=wr_c[:, g].bitcast(FP8X4),
+                    lhsT_scale=wr_s[:, g],
+                    rhs=xc[n][:, g].bitcast(FP8X4),
+                    rhs_scale=xsc[n][:, g],
+                    start=(g == 0),
+                    stop=(g == G - 1),
+                )
+
+        def bias(n):
+            if n >= N_STEPS:
+                return
+            lT_sb[n] = sb.tile([P, STEP], F32, name="lT_sb")
+            nc.scalar.activation(out=lT_sb[n][:], in_=sm[n][:, 0], func=ACT.Identity, bias=br_col[:], scale=1.0)
+
+        def l_transpose(n):
+            if not 0 <= n < N_STEPS:
+                return
+            for s in range(SLABS):
+                cols = slice(P * s, P * (s + 1))
+                nc.tensor.transpose(sm[n][:, 1, cols], lT_sb[n][:, cols], ident[:])
+
+        def rowmax(n):
+            if not 0 <= n < N_STEPS:
+                return
+            negmax[n] = sb.tile([P, SLABS], F32, name="negmax")
+            nc.vector.tensor_reduce(
+                out=negmax[n][:],
+                in_=sm[n][:, 1].rearrange("p (s e) -> p s e", s=SLABS),
+                axis=AX.X,
+                op=ALU.max,
+                negate=True,
+            )
+
+        def expo(n):
+            if not 0 <= n < N_STEPS:
+                return
+            ex[n] = sb.tile([P, SLABS, E], F32, name="ex")
+            esum[n] = sb.tile([P, SLABS], F32, name="esum")
+            for s in range(SLABS):
+                nc.scalar.activation(
+                    out=ex[n][:, s],
+                    in_=sm[n][:, 1, P * s : P * (s + 1)],
+                    func=ACT.Exp,
+                    bias=negmax[n][:, s : s + 1],
+                    scale=1.0,
+                    accum_out=esum[n][:, s : s + 1],
+                )
+
+        def recip(n):
+            if not 0 <= n < N_STEPS:
+                return
+            rsum[n] = sb.tile([P, SLABS], F32, name="rsum")
+            nc.vector.reciprocal(out=rsum[n][:], in_=esum[n][:])
+
+        def normalise(n):
+            if not 0 <= n < N_STEPS:
+                return
+            gn[n] = sb.tile([P, SLABS, E], F32, name="gn")
+            for s in range(SLABS):
+                nc.scalar.activation(out=gn[n][:, s], in_=ex[n][:, s], func=ACT.Copy, scale=rsum[n][:, s : s + 1])
+
+        def g_transpose(n):
+            if not 0 <= n < N_STEPS:
+                return
+            for s in range(SLABS):
+                nc.tensor.transpose(sm[n][:, 0, P * s : P * (s + 1)], gn[n][:, s], ident[:])
+
+        def g_copy(n):
+            if not 0 <= n < N_STEPS:
+                return
+            g_sb[n] = sb.tile([P, STEP], F32, name="g_sb")
+            nc.scalar.activation(out=g_sb[n][:], in_=sm[n][:, 0], func=ACT.Copy, scale=float(E))
+
+        def down(n, s):
+            if not 0 <= n < N_STEPS:
+                return
+            t = psum.tile([P, 4, P], F32, name="ub", bufs=2)
+            cols = slice(P * s, P * (s + 1))
+            for c in range(4):
+                for g in range(G):
+                    nc.tensor.matmul_mx(
+                        out=t[:, c],
+                        lhsT=a_c[:, g, P * c : P * (c + 1)].bitcast(FP8X4),
+                        lhsT_scale=a_s[:, g, P * c : P * (c + 1)],
+                        rhs=xc[n][:, g, cols].bitcast(FP8X4),
+                        rhs_scale=xsc[n][:, g, cols],
+                        start=(g == 0),
+                        stop=(g == G - 1),
+                    )
+            ub[n, s] = t
+
+        def gate(n, s):
+            if not 0 <= n < N_STEPS:
+                return
+            if s == 0:
+                zg[n] = sb.tile([P, STEP, 4], BF16, align_bytes=64, name="zg")
+            cols = slice(P * s, P * (s + 1))
+            nc.vector.tensor_tensor(
+                out=zg[n][:, cols],
+                in0=ub[n, s][:].rearrange("p c n -> p n c"),
+                in1=g_sb[n][:, cols].unsqueeze(2).to_broadcast([P, P, 4]),
+                op=ALU.mult,
+            )
+
+        def z_quantize(n):
+            if not 0 <= n < N_STEPS:
+                return
+            zc[n] = sb.tile([P, STEP], U32, align_bytes=64, name="zc")
+            zs[n] = sb.tile([P, STEP], U8, align_bytes=64, name="zs")
+            quantize(zc[n][:], zs[n][:], zg[n][:].rearrange("p n t -> p (n t)"))
+
+        def combine(n):
+            if not 0 <= n < N_STEPS:
+                return
+            yb[n] = psum.tile([P, SLABS, F], F32, name="yb", bufs=1)
+            for s in range(SLABS):
+                cols = slice(P * s, P * (s + 1))
+                for g in range(G):
+                    nc.tensor.matmul_mx(
+                        out=yb[n][:, s],
+                        lhsT=xc[n][:, g, cols].bitcast(FP8X4),
+                        lhsT_scale=xsc[n][:, g, cols],
+                        rhs=w0_c[:, g].bitcast(FP8X4),
+                        rhs_scale=w0_s[:, g],
+                        start=(g == 0),
+                        stop=False,
+                    )
+                nc.tensor.matmul_mx(
+                    out=yb[n][:, s],
+                    lhsT=zc[n][:, cols].bitcast(FP8X4),
+                    lhsT_scale=zs[n][:, cols],
+                    rhs=b_c[:].bitcast(FP8X4),
+                    rhs_scale=b_s[:],
+                    start=False,
+                    stop=True,
+                )
+
+        def store(n):
+            if not 0 <= n < N_STEPS:
+                return
+            y = sb.tile([P, SLABS, F], F32, name="y")
+            nc.scalar.copy(out=y[:], in_=yb[n][:])
+            dst = out[n * STEP : (n + 1) * STEP, :].rearrange("(p s) f -> p s f", s=SLABS)
+            nc.sync.dma_start(out=dst, in_=y[:])
+
+        for n in range(2):
+            for s in range(SLABS):
+                widen(n, s)
+        x_transpose(0, 0)
+        x_transpose(0, 1)
+        nc.vector.tensor_copy(out=wr_g[:], in_=wr_raw[:].rearrange("p g j n -> p g n j"))
+        gp_interleave(w0_g[:, 0], w0_raw[:, 0].rearrange("p j n -> p n j"))
+        gp_interleave(w0_g[:, 1], w0_raw[:, 1].rearrange("p j n -> p n j"))
+        gp_interleave(b_g[:], b_raw[:].rearrange("p j n -> p n j"))
+
+        for n in range(N_STEPS + 3):
+            g_transpose(n - 2)
+            x_transpose(n + 1, 0)
+            l_transpose(n - 1)
+            x_transpose(n + 1, 1)
+            g_copy(n - 2)
+            widen(n + 2, 0)
+            x_scale_mult(n, 0)
+            rowmax(n - 1)
+            expo(n - 1)
+            gate(n - 2, 0)
+            if n == 0:
+                quantize(wr_c[:].rearrange("p g n -> p (g n)"), wr_s[:].rearrange("p g n -> p (g n)"), wr_g[:].rearrange("p g n t -> p (g n t)"))
+            x_scale_mult(n, 1)
+            gate(n - 2, 1)
+            recip(n - 1)
+            if n == 0:
+                a_interleave(0)
+            x_quantize(n)
+            if n == 0:
+                a_interleave(1)
+                quantize(a_c[:, 0], a_s[:, 0], a_g[:, 0].rearrange("p n t -> p (n t)"))
+            if n == 1:
+                quantize(a_c[:, 1], a_s[:, 1], a_g[:, 1].rearrange("p n t -> p (n t)"))
+            if n == 2:
+                quantize(w0_c[:].rearrange("p g n -> p (g n)"), w0_s[:].rearrange("p g n -> p (g n)"), w0_g[:].rearrange("p g n t -> p (g n t)"))
+                quantize(b_c[:], b_s[:], b_g[:].rearrange("p n t -> p (n t)"))
+            z_quantize(n - 2)
+            combine(n - 3)
+            down(n - 1, 0)
+            down(n - 1, 1)
+            logits(n)
+            widen(n + 2, 1)
+            store(n - 3)
+            normalise(n - 1)
+            bias(n)

@@ -91,7 +91,7 @@ def tile_rankwisemoloradenserouter_t_kernel(tc, x_bytes, x_scale, w0, wr, br, a,
                 in_=a_raw[:, g].rearrange("p j (m t) -> p t m j", t=4),
             )
 
-        xw, xt, xg, xc, xsc = {}, {}, {}, {}, {}
+        xw, xt, xi, xg, xc, xsc = {}, {}, {}, {}, {}, {}
         sm, lT_sb, negmax, ex, esum, rsum, gn, g_sb = {}, {}, {}, {}, {}, {}, {}, {}
         ub, zg, zc, zs, yb = {}, {}, {}, {}, {}
 
@@ -114,16 +114,36 @@ def tile_rankwisemoloradenserouter_t_kernel(tc, x_bytes, x_scale, w0, wr, br, a,
                     )
             xt[n, g] = t
 
+        def x_copy(n):
+            if n >= N_STEPS:
+                return
+            xg[n] = sb.tile([P, G, STEP, 4], BF16, align_bytes=64, name="xg")
+            t = sb.tile([P, P, 4], BF16, align_bytes=64, name="xi")
+            nc.scalar.copy(
+                out=t[:].rearrange("p n t -> p (n t)").bitcast(F32).rearrange("p (n u) -> p n u", u=2),
+                in_=xt[n, 1][:, :, P:].rearrange("p u n -> p n u"),
+            )
+            xi[n] = t
+
+        def x_scale_pool(n):
+            if n >= N_STEPS:
+                return
+            nc.gpsimd.tensor_tensor(
+                out=xg[n][:, 1, P:],
+                in0=xi[n][:],
+                in1=xs[:, 1].unsqueeze(1).to_broadcast([P, P, 4]),
+                op=ALU.mult,
+            )
+
         def x_scale_mult(n, g):
             if n >= N_STEPS:
                 return
-            if g == 0:
-                xg[n] = sb.tile([P, G, STEP, 4], BF16, align_bytes=64, name="xg")
+            cnt = STEP if g == 0 else P
             src = xt[n, g][:].rearrange("p u n -> p (u n)").bitcast(BF16)
             nc.vector.tensor_tensor(
-                out=xg[n][:, g].rearrange("p n (u e) -> p n u e", u=2),
-                in0=src.rearrange("p (u n e) -> p n u e", u=2, e=2),
-                in1=xs[:, g].rearrange("p (u e) -> p u e", u=2).unsqueeze(1).to_broadcast([P, STEP, 2, 2]),
+                out=xg[n][:, g, :cnt].rearrange("p n (u e) -> p n u e", u=2),
+                in0=src.rearrange("p (u n e) -> p n u e", u=2, e=2)[:, :cnt],
+                in1=xs[:, g].rearrange("p (u e) -> p u e", u=2).unsqueeze(1).to_broadcast([P, cnt, 2, 2]),
                 op=ALU.mult,
             )
 
@@ -295,44 +315,47 @@ def tile_rankwisemoloradenserouter_t_kernel(tc, x_bytes, x_scale, w0, wr, br, a,
                 widen(n, s)
         x_transpose(0, 0)
         x_transpose(0, 1)
+        x_copy(0)
+        x_scale_pool(0)
         nc.vector.tensor_copy(out=wr_g[:], in_=wr_raw[:].rearrange("p g j n -> p g n j"))
         gp_interleave(w0_g[:, 0], w0_raw[:, 0].rearrange("p j n -> p n j"))
         gp_interleave(w0_g[:, 1], w0_raw[:, 1].rearrange("p j n -> p n j"))
         gp_interleave(b_g[:], b_raw[:].rearrange("p j n -> p n j"))
 
         for n in range(N_STEPS + 3):
-            g_transpose(n - 2)
             x_transpose(n + 1, 0)
+            normalise(n - 2)
             l_transpose(n - 1)
+            g_transpose(n - 2)
             x_transpose(n + 1, 1)
-            g_copy(n - 2)
             widen(n + 2, 0)
+            g_copy(n - 2)
             x_scale_mult(n, 0)
-            rowmax(n - 1)
-            expo(n - 1)
-            gate(n - 2, 0)
             if n == 0:
                 quantize(wr_c[:].rearrange("p g n -> p (g n)"), wr_s[:].rearrange("p g n -> p (g n)"), wr_g[:].rearrange("p g n t -> p (g n t)"))
             x_scale_mult(n, 1)
-            gate(n - 2, 1)
-            recip(n - 1)
+            rowmax(n - 1)
             if n == 0:
                 a_interleave(0)
             x_quantize(n)
             if n == 0:
                 a_interleave(1)
                 quantize(a_c[:, 0], a_s[:, 0], a_g[:, 0].rearrange("p n t -> p (n t)"))
-            if n == 1:
                 quantize(a_c[:, 1], a_s[:, 1], a_g[:, 1].rearrange("p n t -> p (n t)"))
-            if n == 2:
+            if n == 1:
                 quantize(w0_c[:].rearrange("p g n -> p (g n)"), w0_s[:].rearrange("p g n -> p (g n)"), w0_g[:].rearrange("p g n t -> p (g n t)"))
                 quantize(b_c[:], b_s[:], b_g[:].rearrange("p n t -> p (n t)"))
+            x_copy(n + 1)
+            x_scale_pool(n + 1)
+            widen(n + 2, 1)
+            expo(n - 1)
+            gate(n - 2, 0)
+            gate(n - 2, 1)
+            recip(n - 1)
             z_quantize(n - 2)
             combine(n - 3)
+            logits(n)
             down(n - 1, 0)
             down(n - 1, 1)
-            logits(n)
-            widen(n + 2, 1)
             store(n - 3)
-            normalise(n - 1)
             bias(n)

@@ -5,10 +5,13 @@ from concourse.masks import make_identity
 
 T, D, F, E, R = 4096, 1024, 256, 128, 512
 P = 128
-STEP = 256
-N_STEPS = T // STEP
-SLABS = STEP // P
 G = D // 512
+WIDTHS = [256] * 16
+STARTS = [sum(WIDTHS[:n]) for n in range(len(WIDTHS))]
+N_STEPS = len(WIDTHS)
+STEP = max(WIDTHS)
+POOL_TOKENS = 160
+VECTOR_COLUMNS = 256
 FLOPS = 2 * T * D * (F + E + R) + 2 * T * R * F
 
 F32 = mybir.dt.float32
@@ -27,16 +30,18 @@ def tile_rankwisemoloradenserouter_t_kernel(tc, x_bytes, x_scale, w0, wr, br, a,
     with ExitStack() as ctx:
         keep = ctx.enter_context(tc.tile_pool(name="keep", bufs=1))
         bytes_pool = ctx.enter_context(tc.tile_pool(name="xbytes", bufs=N_STEPS))
-        sb = ctx.enter_context(tc.tile_pool(name="sb", bufs=3))
+        sb = ctx.enter_context(tc.tile_pool(name="sb", bufs=5))
         psum = ctx.enter_context(tc.psum_pool(name="psum", bufs=2))
         ctx.enter_context(tc.manual_schedule())
 
         xb = {}
 
+        def rows(ap, n):
+            return ap[STARTS[n] : STARTS[n] + WIDTHS[n], :].rearrange("(p s) k -> p s k", s=WIDTHS[n] // P)
+
         def load_x(n):
-            t = bytes_pool.tile([P, SLABS, D], U8, name="xb")
-            src = x_bytes[n * STEP : (n + 1) * STEP, :].rearrange("(p s) k -> p s k", s=SLABS)
-            nc.sync.dma_start(out=t[:], in_=src)
+            t = bytes_pool.tile([P, WIDTHS[n] // P, D], U8, name="xb")
+            nc.sync.dma_start(out=t[:], in_=rows(x_bytes, n))
             xb[n] = t
 
         wr_raw = keep.tile([P, G, 4, E], BF16, name="wr_raw")
@@ -48,16 +53,17 @@ def tile_rankwisemoloradenserouter_t_kernel(tc, x_bytes, x_scale, w0, wr, br, a,
 
         load_x(0)
         nc.sync.dma_start(out=wr_raw[:], in_=wr.rearrange("(g p j) n -> p g j n", g=G, j=4))
+        load_x(1)
         nc.sync.dma_start(out=xs[:], in_=x_scale.rearrange("o (g p t) -> p (o g) t", g=G, t=4))
         with nc.allow_non_contiguous_dma(reason="one bias value to a partition"):
             nc.sync.dma_start(out=br_col[:], in_=br.rearrange("(p o) -> p o", o=1))
-        load_x(1)
+        load_x(2)
         for g in range(G):
             nc.sync.dma_start(out=a_raw[:, g], in_=a[512 * g : 512 * (g + 1), :].rearrange("(p j) n -> p j n", j=4))
-        load_x(2)
+        load_x(3)
         nc.sync.dma_start(out=w0_raw[:], in_=w0.rearrange("(g p j) n -> p g j n", g=G, j=4))
         nc.sync.dma_start(out=b_raw[:], in_=b.rearrange("(p j) n -> p j n", j=4))
-        for n in range(3, N_STEPS):
+        for n in range(4, N_STEPS):
             load_x(n)
 
         warm = keep.tile([P, 1], F32, name="warm")
@@ -82,76 +88,100 @@ def tile_rankwisemoloradenserouter_t_kernel(tc, x_bytes, x_scale, w0, wr, br, a,
         def quantize(codes, scales, grouped):
             nc.vector.quantize_mx(out=codes.bitcast(FP8X4), scales=scales, in_=grouped)
 
-        def gp_interleave(dst, src):
+        def pool_copy(dst, src):
             nc.gpsimd.tensor_scalar(dst, src, 1.0, 0.0, op0=ALU.mult, op1=ALU.add)
-
-        def a_interleave(g):
-            nc.vector.tensor_copy(
-                out=a_g[:, g].rearrange("p (t m) j -> p t m j", t=4),
-                in_=a_raw[:, g].rearrange("p j (m t) -> p t m j", t=4),
-            )
 
         xw, xt, xi, xg, xc, xsc = {}, {}, {}, {}, {}, {}
         sm, lT_sb, negmax, ex, esum, rsum, gn, g_sb = {}, {}, {}, {}, {}, {}, {}, {}
         ub, zg, zc, zs, yb = {}, {}, {}, {}, {}
 
+        def valid(n, s=0):
+            return 0 <= n < N_STEPS and P * s < WIDTHS[n]
+
+        def slabs(n):
+            return range(WIDTHS[n] // P)
+
+        def cols(s):
+            return slice(P * s, P * (s + 1))
+
+        def pool_tokens(n):
+            return POOL_TOKENS if n > 0 and WIDTHS[n] == STEP else 0
+
         def widen(n, s):
-            if n >= N_STEPS:
+            if not valid(n, s):
                 return
-            if s == 0:
-                xw[n] = sb.tile([P, SLABS, D], BF16, name="xw")
-            nc.scalar.copy(out=xw[n][:, s], in_=xb[n][:, s].bitcast(FP8))
+            if n not in xw:
+                xw[n] = sb.tile([P, WIDTHS[n] // P, D], BF16, name="xw", bufs=8)
+            if (n, s) in ((0, 1), (1, 1)):
+                nc.vector.tensor_copy(out=xw[n][:, s], in_=xb[n][:, s].bitcast(FP8))
+            else:
+                first = VECTOR_COLUMNS if n > 1 and s == 1 else 0
+                nc.scalar.copy(out=xw[n][:, s, first:], in_=xb[n][:, s, first:].bitcast(FP8))
+
+        def widen_vector(n):
+            if not valid(n, 1) or n < 2:
+                return
+            if n not in xw:
+                xw[n] = sb.tile([P, WIDTHS[n] // P, D], BF16, name="xw", bufs=8)
+            nc.vector.tensor_copy(
+                out=xw[n][:, 1, :VECTOR_COLUMNS], in_=xb[n][:, 1, :VECTOR_COLUMNS].bitcast(FP8)
+            )
 
         def x_transpose(n, g):
-            if n >= N_STEPS:
+            if not valid(n):
                 return
-            t = psum.tile([P, 2, STEP], F32, name="xt", bufs=3)
-            for s in range(SLABS):
+            t = psum.tile([P, 2, WIDTHS[n]], F32, name="xt", bufs=3)
+            for s in slabs(n):
                 words = xw[n][:, s].bitcast(F32)
                 for u in range(2):
-                    nc.tensor.transpose(
-                        t[:, u, P * s : P * (s + 1)], words[:, 256 * g + u : 256 * (g + 1) : 2], ident[:]
-                    )
+                    nc.tensor.transpose(t[:, u, cols(s)], words[:, 256 * g + u : 256 * (g + 1) : 2], ident[:])
             xt[n, g] = t
 
+        def new_xg(n):
+            if n not in xg:
+                xg[n] = sb.tile([P, G, WIDTHS[n], 4], BF16, align_bytes=64, name="xg")
+
         def x_copy(n):
-            if n >= N_STEPS:
+            if not valid(n) or not pool_tokens(n):
                 return
-            xg[n] = sb.tile([P, G, STEP, 4], BF16, align_bytes=64, name="xg")
-            t = sb.tile([P, P, 4], BF16, align_bytes=64, name="xi")
+            first = WIDTHS[n] - pool_tokens(n)
+            t = sb.tile([P, pool_tokens(n), 4], BF16, align_bytes=64, name="xi")
             nc.scalar.copy(
                 out=t[:].rearrange("p n t -> p (n t)").bitcast(F32).rearrange("p (n u) -> p n u", u=2),
-                in_=xt[n, 1][:, :, P:].rearrange("p u n -> p n u"),
+                in_=xt[n, 1][:, :, first:].rearrange("p u n -> p n u"),
             )
             xi[n] = t
 
         def x_scale_pool(n):
-            if n >= N_STEPS:
+            if not valid(n) or not pool_tokens(n):
                 return
+            new_xg(n)
+            count = pool_tokens(n)
             nc.gpsimd.tensor_tensor(
-                out=xg[n][:, 1, P:],
+                out=xg[n][:, 1, WIDTHS[n] - count :],
                 in0=xi[n][:],
-                in1=xs[:, 1].unsqueeze(1).to_broadcast([P, P, 4]),
+                in1=xs[:, 1].unsqueeze(1).to_broadcast([P, count, 4]),
                 op=ALU.mult,
             )
 
-        def x_scale_mult(n, g):
-            if n >= N_STEPS:
+        def x_scale_vector(n, g):
+            if not valid(n):
                 return
-            cnt = STEP if g == 0 else P
-            src = xt[n, g][:].rearrange("p u n -> p (u n)").bitcast(BF16)
+            new_xg(n)
+            count = WIDTHS[n] - (pool_tokens(n) if g == 1 else 0)
+            values = xt[n, g][:].rearrange("p u n -> p (u n)").bitcast(BF16)
             nc.vector.tensor_tensor(
-                out=xg[n][:, g, :cnt].rearrange("p n (u e) -> p n u e", u=2),
-                in0=src.rearrange("p (u n e) -> p n u e", u=2, e=2)[:, :cnt],
-                in1=xs[:, g].rearrange("p (u e) -> p u e", u=2).unsqueeze(1).to_broadcast([P, cnt, 2, 2]),
+                out=xg[n][:, g, :count].rearrange("p n (u e) -> p n u e", u=2),
+                in0=values.rearrange("p (u n e) -> p n u e", u=2, e=2)[:, :count],
+                in1=xs[:, g].rearrange("p (u e) -> p u e", u=2).unsqueeze(1).to_broadcast([P, count, 2, 2]),
                 op=ALU.mult,
             )
 
         def x_quantize(n):
-            if n >= N_STEPS:
+            if not valid(n):
                 return
-            xc[n] = sb.tile([P, G, STEP], U32, align_bytes=64, name="xc", bufs=6)
-            xsc[n] = sb.tile([P, G, STEP], U8, align_bytes=64, name="xsc", bufs=6)
+            xc[n] = sb.tile([P, G, WIDTHS[n]], U32, align_bytes=64, name="xc", bufs=10)
+            xsc[n] = sb.tile([P, G, WIDTHS[n]], U8, align_bytes=64, name="xsc", bufs=10)
             quantize(
                 xc[n][:].rearrange("p g n -> p (g n)"),
                 xsc[n][:].rearrange("p g n -> p (g n)"),
@@ -159,12 +189,12 @@ def tile_rankwisemoloradenserouter_t_kernel(tc, x_bytes, x_scale, w0, wr, br, a,
             )
 
         def logits(n):
-            if n >= N_STEPS:
+            if not valid(n):
                 return
             sm[n] = psum.tile([P, 2, STEP], F32, name="sm")
             for g in range(G):
                 nc.tensor.matmul_mx(
-                    out=sm[n][:, 0],
+                    out=sm[n][:, 0, : WIDTHS[n]],
                     lhsT=wr_c[:, g].bitcast(FP8X4),
                     lhsT_scale=wr_s[:, g],
                     rhs=xc[n][:, g].bitcast(FP8X4),
@@ -174,39 +204,40 @@ def tile_rankwisemoloradenserouter_t_kernel(tc, x_bytes, x_scale, w0, wr, br, a,
                 )
 
         def bias(n):
-            if n >= N_STEPS:
+            if not valid(n):
                 return
-            lT_sb[n] = sb.tile([P, STEP], F32, name="lT_sb")
-            nc.scalar.activation(out=lT_sb[n][:], in_=sm[n][:, 0], func=ACT.Identity, bias=br_col[:], scale=1.0)
+            lT_sb[n] = sb.tile([P, WIDTHS[n]], F32, name="lT_sb")
+            nc.scalar.activation(
+                out=lT_sb[n][:], in_=sm[n][:, 0, : WIDTHS[n]], func=ACT.Identity, bias=br_col[:], scale=1.0
+            )
 
         def l_transpose(n):
-            if not 0 <= n < N_STEPS:
+            if not valid(n):
                 return
-            for s in range(SLABS):
-                cols = slice(P * s, P * (s + 1))
-                nc.tensor.transpose(sm[n][:, 1, cols], lT_sb[n][:, cols], ident[:])
+            for s in slabs(n):
+                nc.tensor.transpose(sm[n][:, 1, cols(s)], lT_sb[n][:, cols(s)], ident[:])
 
         def rowmax(n):
-            if not 0 <= n < N_STEPS:
+            if not valid(n):
                 return
-            negmax[n] = sb.tile([P, SLABS], F32, name="negmax")
+            negmax[n] = sb.tile([P, WIDTHS[n] // P], F32, name="negmax")
             nc.vector.tensor_reduce(
                 out=negmax[n][:],
-                in_=sm[n][:, 1].rearrange("p (s e) -> p s e", s=SLABS),
+                in_=sm[n][:, 1, : WIDTHS[n]].rearrange("p (s e) -> p s e", e=E),
                 axis=AX.X,
                 op=ALU.max,
                 negate=True,
             )
 
         def expo(n):
-            if not 0 <= n < N_STEPS:
+            if not valid(n):
                 return
-            ex[n] = sb.tile([P, SLABS, E], F32, name="ex")
-            esum[n] = sb.tile([P, SLABS], F32, name="esum")
-            for s in range(SLABS):
+            ex[n] = sb.tile([P, WIDTHS[n] // P, E], F32, name="ex")
+            esum[n] = sb.tile([P, WIDTHS[n] // P], F32, name="esum")
+            for s in slabs(n):
                 nc.scalar.activation(
                     out=ex[n][:, s],
-                    in_=sm[n][:, 1, P * s : P * (s + 1)],
+                    in_=sm[n][:, 1, cols(s)],
                     func=ACT.Exp,
                     bias=negmax[n][:, s : s + 1],
                     scale=1.0,
@@ -214,79 +245,78 @@ def tile_rankwisemoloradenserouter_t_kernel(tc, x_bytes, x_scale, w0, wr, br, a,
                 )
 
         def recip(n):
-            if not 0 <= n < N_STEPS:
+            if not valid(n):
                 return
-            rsum[n] = sb.tile([P, SLABS], F32, name="rsum")
+            rsum[n] = sb.tile([P, WIDTHS[n] // P], F32, name="rsum")
             nc.vector.reciprocal(out=rsum[n][:], in_=esum[n][:])
 
         def normalise(n):
-            if not 0 <= n < N_STEPS:
+            if not valid(n):
                 return
-            gn[n] = sb.tile([P, SLABS, E], F32, name="gn")
-            for s in range(SLABS):
-                nc.scalar.activation(out=gn[n][:, s], in_=ex[n][:, s], func=ACT.Copy, scale=rsum[n][:, s : s + 1])
+            gn[n] = sb.tile([P, WIDTHS[n] // P, E], F32, name="gn")
+            for s in slabs(n):
+                nc.gpsimd.tensor_scalar(
+                    gn[n][:, s], ex[n][:, s], rsum[n][:, s : s + 1], float(E), op0=ALU.mult, op1=ALU.mult
+                )
 
         def g_transpose(n):
-            if not 0 <= n < N_STEPS:
+            if not valid(n):
                 return
-            for s in range(SLABS):
-                nc.tensor.transpose(sm[n][:, 0, P * s : P * (s + 1)], gn[n][:, s], ident[:])
+            for s in slabs(n):
+                nc.tensor.transpose(sm[n][:, 0, cols(s)], gn[n][:, s], ident[:])
 
         def g_copy(n):
-            if not 0 <= n < N_STEPS:
+            if not valid(n):
                 return
-            g_sb[n] = sb.tile([P, STEP], F32, name="g_sb")
-            nc.scalar.activation(out=g_sb[n][:], in_=sm[n][:, 0], func=ACT.Copy, scale=float(E))
+            g_sb[n] = sb.tile([P, WIDTHS[n]], F32, name="g_sb")
+            nc.scalar.copy(out=g_sb[n][:], in_=sm[n][:, 0, : WIDTHS[n]])
 
         def down(n, s):
-            if not 0 <= n < N_STEPS:
+            if not valid(n, s):
                 return
-            t = psum.tile([P, 4, P], F32, name="ub", bufs=2)
-            cols = slice(P * s, P * (s + 1))
+            t = psum.tile([P, 4, P], F32, name="ub")
             for c in range(4):
                 for g in range(G):
                     nc.tensor.matmul_mx(
                         out=t[:, c],
-                        lhsT=a_c[:, g, P * c : P * (c + 1)].bitcast(FP8X4),
-                        lhsT_scale=a_s[:, g, P * c : P * (c + 1)],
-                        rhs=xc[n][:, g, cols].bitcast(FP8X4),
-                        rhs_scale=xsc[n][:, g, cols],
+                        lhsT=a_c[:, g, cols(c)].bitcast(FP8X4),
+                        lhsT_scale=a_s[:, g, cols(c)],
+                        rhs=xc[n][:, g, cols(s)].bitcast(FP8X4),
+                        rhs_scale=xsc[n][:, g, cols(s)],
                         start=(g == 0),
                         stop=(g == G - 1),
                     )
             ub[n, s] = t
 
         def gate(n, s):
-            if not 0 <= n < N_STEPS:
+            if not valid(n, s):
                 return
-            if s == 0:
-                zg[n] = sb.tile([P, STEP, 4], BF16, align_bytes=64, name="zg")
-            cols = slice(P * s, P * (s + 1))
+            if n not in zg:
+                zg[n] = sb.tile([P, WIDTHS[n], 4], BF16, align_bytes=64, name="zg")
             nc.vector.tensor_tensor(
-                out=zg[n][:, cols],
+                out=zg[n][:, cols(s)],
                 in0=ub[n, s][:].rearrange("p c n -> p n c"),
-                in1=g_sb[n][:, cols].unsqueeze(2).to_broadcast([P, P, 4]),
+                in1=g_sb[n][:, cols(s)].unsqueeze(2).to_broadcast([P, P, 4]),
                 op=ALU.mult,
             )
 
         def z_quantize(n):
-            if not 0 <= n < N_STEPS:
+            if not valid(n):
                 return
-            zc[n] = sb.tile([P, STEP], U32, align_bytes=64, name="zc")
-            zs[n] = sb.tile([P, STEP], U8, align_bytes=64, name="zs")
+            zc[n] = sb.tile([P, WIDTHS[n]], U32, align_bytes=64, name="zc")
+            zs[n] = sb.tile([P, WIDTHS[n]], U8, align_bytes=64, name="zs")
             quantize(zc[n][:], zs[n][:], zg[n][:].rearrange("p n t -> p (n t)"))
 
         def combine(n):
-            if not 0 <= n < N_STEPS:
+            if not valid(n):
                 return
-            yb[n] = psum.tile([P, SLABS, F], F32, name="yb", bufs=1)
-            for s in range(SLABS):
-                cols = slice(P * s, P * (s + 1))
+            yb[n] = psum.tile([P, WIDTHS[n] // P, F], F32, name="yb", bufs=1)
+            for s in slabs(n):
                 for g in range(G):
                     nc.tensor.matmul_mx(
                         out=yb[n][:, s],
-                        lhsT=xc[n][:, g, cols].bitcast(FP8X4),
-                        lhsT_scale=xsc[n][:, g, cols],
+                        lhsT=xc[n][:, g, cols(s)].bitcast(FP8X4),
+                        lhsT_scale=xsc[n][:, g, cols(s)],
                         rhs=w0_c[:, g].bitcast(FP8X4),
                         rhs_scale=w0_s[:, g],
                         start=(g == 0),
@@ -294,8 +324,8 @@ def tile_rankwisemoloradenserouter_t_kernel(tc, x_bytes, x_scale, w0, wr, br, a,
                     )
                 nc.tensor.matmul_mx(
                     out=yb[n][:, s],
-                    lhsT=zc[n][:, cols].bitcast(FP8X4),
-                    lhsT_scale=zs[n][:, cols],
+                    lhsT=zc[n][:, cols(s)].bitcast(FP8X4),
+                    lhsT_scale=zs[n][:, cols(s)],
                     rhs=b_c[:].bitcast(FP8X4),
                     rhs_scale=b_s[:],
                     start=False,
@@ -303,59 +333,97 @@ def tile_rankwisemoloradenserouter_t_kernel(tc, x_bytes, x_scale, w0, wr, br, a,
                 )
 
         def store(n):
-            if not 0 <= n < N_STEPS:
+            if not valid(n):
                 return
-            y = sb.tile([P, SLABS, F], F32, name="y")
+            y = sb.tile([P, WIDTHS[n] // P, F], F32, name="y")
             nc.scalar.copy(out=y[:], in_=yb[n][:])
-            dst = out[n * STEP : (n + 1) * STEP, :].rearrange("(p s) f -> p s f", s=SLABS)
-            nc.sync.dma_start(out=dst, in_=y[:])
+            nc.sync.dma_start(out=rows(out, n), in_=y[:])
 
-        for n in range(2):
-            for s in range(SLABS):
-                widen(n, s)
-        x_transpose(0, 0)
-        x_transpose(0, 1)
-        x_copy(0)
-        x_scale_pool(0)
-        nc.vector.tensor_copy(out=wr_g[:], in_=wr_raw[:].rearrange("p g j n -> p g n j"))
-        gp_interleave(w0_g[:, 0], w0_raw[:, 0].rearrange("p j n -> p n j"))
-        gp_interleave(w0_g[:, 1], w0_raw[:, 1].rearrange("p j n -> p n j"))
-        gp_interleave(b_g[:], b_raw[:].rearrange("p j n -> p n j"))
+        def wr_group():
+            nc.vector.tensor_copy(out=wr_g[:], in_=wr_raw[:].rearrange("p g j n -> p g n j"))
 
-        for n in range(N_STEPS + 3):
-            x_transpose(n + 1, 0)
-            normalise(n - 2)
-            l_transpose(n - 1)
-            g_transpose(n - 2)
-            x_transpose(n + 1, 1)
-            widen(n + 2, 0)
-            g_copy(n - 2)
-            x_scale_mult(n, 0)
-            if n == 0:
-                quantize(wr_c[:].rearrange("p g n -> p (g n)"), wr_s[:].rearrange("p g n -> p (g n)"), wr_g[:].rearrange("p g n t -> p (g n t)"))
-            x_scale_mult(n, 1)
-            rowmax(n - 1)
-            if n == 0:
-                a_interleave(0)
-            x_quantize(n)
-            if n == 0:
-                a_interleave(1)
-                quantize(a_c[:, 0], a_s[:, 0], a_g[:, 0].rearrange("p n t -> p (n t)"))
-                quantize(a_c[:, 1], a_s[:, 1], a_g[:, 1].rearrange("p n t -> p (n t)"))
-            if n == 1:
-                quantize(w0_c[:].rearrange("p g n -> p (g n)"), w0_s[:].rearrange("p g n -> p (g n)"), w0_g[:].rearrange("p g n t -> p (g n t)"))
-                quantize(b_c[:], b_s[:], b_g[:].rearrange("p n t -> p (n t)"))
-            x_copy(n + 1)
-            x_scale_pool(n + 1)
-            widen(n + 2, 1)
-            expo(n - 1)
+        def wr_quantize():
+            quantize(
+                wr_c[:].rearrange("p g n -> p (g n)"),
+                wr_s[:].rearrange("p g n -> p (g n)"),
+                wr_g[:].rearrange("p g n t -> p (g n t)"),
+            )
+
+        def a_group(g):
+            dst = a_g[:, g].rearrange("p (t m) j -> p t m j", t=4)
+            src = a_raw[:, g].rearrange("p j (m t) -> p t m j", t=4)
+            if g == 0:
+                for c in range(4):
+                    pool_copy(dst[:, c], src[:, c])
+            else:
+                nc.vector.tensor_copy(out=dst, in_=src)
+
+        def a_quantize(g):
+            quantize(a_c[:, g], a_s[:, g], a_g[:, g].rearrange("p n t -> p (n t)"))
+
+        def w0_group():
+            for g in range(G):
+                for h in range(2):
+                    pool_copy(w0_g[:, g, cols(h)], w0_raw[:, g, :, cols(h)].rearrange("p j n -> p n j"))
+
+        def w0_quantize():
+            quantize(
+                w0_c[:].rearrange("p g n -> p (g n)"),
+                w0_s[:].rearrange("p g n -> p (g n)"),
+                w0_g[:].rearrange("p g n t -> p (g n t)"),
+            )
+
+        def b_group():
+            for h in range(2):
+                pool_copy(b_g[:, cols(h)], b_raw[:, :, cols(h)].rearrange("p j n -> p n j"))
+
+        def b_quantize():
+            quantize(b_c[:], b_s[:], b_g[:].rearrange("p n t -> p (n t)"))
+
+        for n in range(-4, N_STEPS + 3):
             gate(n - 2, 0)
-            gate(n - 2, 1)
+            expo(n - 1)
             recip(n - 1)
-            z_quantize(n - 2)
-            combine(n - 3)
+            gate(n - 2, 1)
+            widen_vector(n + 3)
             logits(n)
             down(n - 1, 0)
-            down(n - 1, 1)
-            store(n - 3)
+            if n == -1:
+                wr_quantize()
+            if n == 2:
+                w0_group()
+            x_transpose(n + 2, 1)
+            x_scale_vector(n + 1, 1)
+            if n == 1:
+                b_group()
+            normalise(n - 1)
+            if n == 0:
+                a_group(0)
+            x_scale_vector(n + 1, 0)
+            widen(n + 4, 0)
             bias(n)
+            g_transpose(n - 1)
+            if n == 0:
+                a_quantize(0)
+            if n == 0:
+                a_quantize(1)
+            widen(n + 3, 1)
+            l_transpose(n)
+            if n == -3:
+                wr_group()
+            if n == 2:
+                b_quantize()
+            x_transpose(n + 2, 0)
+            store(n - 3)
+            z_quantize(n - 2)
+            g_copy(n - 1)
+            down(n - 1, 1)
+            rowmax(n)
+            if n == -1:
+                a_group(1)
+            if n == 2:
+                w0_quantize()
+            x_scale_pool(n + 1)
+            x_copy(n + 2)
+            x_quantize(n + 1)
+            combine(n - 2)

@@ -5,13 +5,14 @@ from concourse.masks import make_identity
 
 T, D, F, E, R = 4096, 1024, 256, 128, 512
 P = 128
-G = D // 512
-WIDTHS = [256] * 16
-STARTS = [sum(WIDTHS[:n]) for n in range(len(WIDTHS))]
-N_STEPS = len(WIDTHS)
-STEP = max(WIDTHS)
-POOL_TOKENS = 160
-VECTOR_COLUMNS = 256
+PACK = 4
+GROUPS = D // (P * PACK)
+STEP = 256
+N_STEPS = T // STEP
+SLABS = STEP // P
+POOL_TOKENS = 128
+WIDENED_ON_VECTOR = ((0, 1), (1, 1))
+
 FLOPS = 2 * T * D * (F + E + R) + 2 * T * R * F
 
 F32 = mybir.dt.float32
@@ -34,35 +35,38 @@ def tile_rankwisemoloradenserouter_t_kernel(tc, x_bytes, x_scale, w0, wr, br, a,
         psum = ctx.enter_context(tc.psum_pool(name="psum", bufs=2))
         ctx.enter_context(tc.manual_schedule())
 
+        def rows(ap, n):
+            return ap[n * STEP : (n + 1) * STEP, :].rearrange("(p s) k -> p s k", s=SLABS)
+
+        def cols(i):
+            return slice(P * i, P * (i + 1))
+
         xb = {}
 
-        def rows(ap, n):
-            return ap[STARTS[n] : STARTS[n] + WIDTHS[n], :].rearrange("(p s) k -> p s k", s=WIDTHS[n] // P)
-
         def load_x(n):
-            t = bytes_pool.tile([P, WIDTHS[n] // P, D], U8, name="xb")
-            nc.sync.dma_start(out=t[:], in_=rows(x_bytes, n))
-            xb[n] = t
+            xb[n] = bytes_pool.tile([P, SLABS, D], U8, name="xb")
+            nc.sync.dma_start(out=xb[n][:], in_=rows(x_bytes, n))
 
-        wr_raw = keep.tile([P, G, 4, E], BF16, name="wr_raw")
-        a_raw = keep.tile([P, G, 4, R], BF16, name="a_raw")
-        w0_raw = keep.tile([P, G, 4, F], BF16, name="w0_raw")
-        b_raw = keep.tile([P, 4, F], BF16, name="b_raw")
-        xs = keep.tile([P, G, 4], F32, name="xs")
+        wr_raw = keep.tile([P, GROUPS, PACK, E], BF16, name="wr_raw")
+        a_raw = keep.tile([P, GROUPS, PACK, R], BF16, name="a_raw")
+        w0_raw = keep.tile([P, GROUPS, PACK, F], BF16, name="w0_raw")
+        b_raw = keep.tile([P, PACK, F], BF16, name="b_raw")
+        xs = keep.tile([P, GROUPS, PACK], F32, name="xs")
         br_col = keep.tile([P, 1], BF16, name="br_col")
 
         load_x(0)
-        nc.sync.dma_start(out=wr_raw[:], in_=wr.rearrange("(g p j) n -> p g j n", g=G, j=4))
+        nc.sync.dma_start(out=wr_raw[:], in_=wr.rearrange("(g p j) n -> p g j n", g=GROUPS, j=PACK))
         load_x(1)
-        nc.sync.dma_start(out=xs[:], in_=x_scale.rearrange("o (g p t) -> p (o g) t", g=G, t=4))
+        nc.sync.dma_start(out=xs[:], in_=x_scale.rearrange("o (g p t) -> p (o g) t", g=GROUPS, t=PACK))
         with nc.allow_non_contiguous_dma(reason="one bias value to a partition"):
             nc.sync.dma_start(out=br_col[:], in_=br.rearrange("(p o) -> p o", o=1))
         load_x(2)
-        for g in range(G):
-            nc.sync.dma_start(out=a_raw[:, g], in_=a[512 * g : 512 * (g + 1), :].rearrange("(p j) n -> p j n", j=4))
+        for g in range(GROUPS):
+            a_rows = a[P * PACK * g : P * PACK * (g + 1), :]
+            nc.sync.dma_start(out=a_raw[:, g], in_=a_rows.rearrange("(p j) n -> p j n", j=PACK))
         load_x(3)
-        nc.sync.dma_start(out=w0_raw[:], in_=w0.rearrange("(g p j) n -> p g j n", g=G, j=4))
-        nc.sync.dma_start(out=b_raw[:], in_=b.rearrange("(p j) n -> p j n", j=4))
+        nc.sync.dma_start(out=w0_raw[:], in_=w0.rearrange("(g p j) n -> p g j n", g=GROUPS, j=PACK))
+        nc.sync.dma_start(out=b_raw[:], in_=b.rearrange("(p j) n -> p j n", j=PACK))
         for n in range(4, N_STEPS):
             load_x(n)
 
@@ -72,106 +76,135 @@ def tile_rankwisemoloradenserouter_t_kernel(tc, x_bytes, x_scale, w0, wr, br, a,
         ident = keep.tile([P, P], F32, name="ident")
         make_identity(nc, ident[:])
 
-        wr_g = keep.tile([P, G, E, 4], BF16, align_bytes=64, name="wr_g")
-        a_g = keep.tile([P, G, R, 4], BF16, align_bytes=64, name="a_g")
-        w0_g = keep.tile([P, G, F, 4], BF16, align_bytes=64, name="w0_g")
-        b_g = keep.tile([P, F, 4], BF16, align_bytes=64, name="b_g")
-        wr_c = keep.tile([P, G, E], U32, align_bytes=64, name="wr_c")
-        wr_s = keep.tile([P, G, E], U8, align_bytes=64, name="wr_s")
-        a_c = keep.tile([P, G, R], U32, align_bytes=64, name="a_c")
-        a_s = keep.tile([P, G, R], U8, align_bytes=64, name="a_s")
-        w0_c = keep.tile([P, G, F], U32, align_bytes=64, name="w0_c")
-        w0_s = keep.tile([P, G, F], U8, align_bytes=64, name="w0_s")
+        wr_g = keep.tile([P, GROUPS, E, PACK], BF16, align_bytes=64, name="wr_g")
+        a_g = keep.tile([P, GROUPS, R, PACK], BF16, align_bytes=64, name="a_g")
+        w0_g = keep.tile([P, GROUPS, F, PACK], BF16, align_bytes=64, name="w0_g")
+        b_g = keep.tile([P, F, PACK], BF16, align_bytes=64, name="b_g")
+        wr_c = keep.tile([P, GROUPS, E], U32, align_bytes=64, name="wr_c")
+        wr_s = keep.tile([P, GROUPS, E], U8, align_bytes=64, name="wr_s")
+        a_c = keep.tile([P, GROUPS, R], U32, align_bytes=64, name="a_c")
+        a_s = keep.tile([P, GROUPS, R], U8, align_bytes=64, name="a_s")
+        w0_c = keep.tile([P, GROUPS, F], U32, align_bytes=64, name="w0_c")
+        w0_s = keep.tile([P, GROUPS, F], U8, align_bytes=64, name="w0_s")
         b_c = keep.tile([P, F], U32, align_bytes=64, name="b_c")
         b_s = keep.tile([P, F], U8, align_bytes=64, name="b_s")
 
-        def quantize(codes, scales, grouped):
-            nc.vector.quantize_mx(out=codes.bitcast(FP8X4), scales=scales, in_=grouped)
+        def quantize(codes, scales, packed):
+            nc.vector.quantize_mx(out=codes.bitcast(FP8X4), scales=scales, in_=packed)
 
         def pool_copy(dst, src):
             nc.gpsimd.tensor_scalar(dst, src, 1.0, 0.0, op0=ALU.mult, op1=ALU.add)
 
+        def wr_pack():
+            nc.vector.tensor_copy(out=wr_g[:], in_=wr_raw[:].rearrange("p g j n -> p g n j"))
+
+        def wr_quantize():
+            quantize(
+                wr_c[:].rearrange("p g n -> p (g n)"),
+                wr_s[:].rearrange("p g n -> p (g n)"),
+                wr_g[:].rearrange("p g n t -> p (g n t)"),
+            )
+
+        def a_pack(g):
+            dst = a_g[:, g].rearrange("p (c m) j -> p c m j", c=PACK)
+            src = a_raw[:, g].rearrange("p j (m c) -> p c m j", c=PACK)
+            if g == 0:
+                for c in range(PACK):
+                    pool_copy(dst[:, c], src[:, c])
+            else:
+                nc.vector.tensor_copy(out=dst, in_=src)
+
+        def a_quantize(g):
+            quantize(a_c[:, g], a_s[:, g], a_g[:, g].rearrange("p n t -> p (n t)"))
+
+        def w0_pack():
+            for g in range(GROUPS):
+                for h in range(F // P):
+                    pool_copy(w0_g[:, g, cols(h)], w0_raw[:, g, :, cols(h)].rearrange("p j n -> p n j"))
+
+        def w0_quantize():
+            quantize(
+                w0_c[:].rearrange("p g n -> p (g n)"),
+                w0_s[:].rearrange("p g n -> p (g n)"),
+                w0_g[:].rearrange("p g n t -> p (g n t)"),
+            )
+
+        def b_pack():
+            for h in range(F // P):
+                pool_copy(b_g[:, cols(h)], b_raw[:, :, cols(h)].rearrange("p j n -> p n j"))
+
+        def b_quantize():
+            quantize(b_c[:], b_s[:], b_g[:].rearrange("p n t -> p (n t)"))
+
         xw, xt, xi, xg, xc, xsc = {}, {}, {}, {}, {}, {}
-        sm, lT_sb, negmax, ex, esum, rsum, gn, g_sb = {}, {}, {}, {}, {}, {}, {}, {}
+        sm, lT, negmax, ex, esum, rsum, gn, gT = {}, {}, {}, {}, {}, {}, {}, {}
         ub, zg, zc, zs, yb = {}, {}, {}, {}, {}
 
-        def valid(n, s=0):
-            return 0 <= n < N_STEPS and P * s < WIDTHS[n]
-
-        def slabs(n):
-            return range(WIDTHS[n] // P)
-
-        def cols(s):
-            return slice(P * s, P * (s + 1))
+        def valid(n):
+            return 0 <= n < N_STEPS
 
         def pool_tokens(n):
-            return POOL_TOKENS if n > 0 and WIDTHS[n] == STEP else 0
+            return POOL_TOKENS if n > 0 else 0
 
         def widen(n, s):
-            if not valid(n, s):
+            if not valid(n):
                 return
             if n not in xw:
-                xw[n] = sb.tile([P, WIDTHS[n] // P, D], BF16, name="xw", bufs=8)
-            if (n, s) in ((0, 1), (1, 1)):
-                nc.vector.tensor_copy(out=xw[n][:, s], in_=xb[n][:, s].bitcast(FP8))
+                xw[n] = sb.tile([P, SLABS, D], BF16, name="xw")
+            codes = xb[n][:, s].bitcast(FP8)
+            if (n, s) in WIDENED_ON_VECTOR:
+                nc.vector.tensor_copy(out=xw[n][:, s], in_=codes)
             else:
-                first = VECTOR_COLUMNS if n > 1 and s == 1 else 0
-                nc.scalar.copy(out=xw[n][:, s, first:], in_=xb[n][:, s, first:].bitcast(FP8))
-
-        def widen_vector(n):
-            if not valid(n, 1) or n < 2:
-                return
-            if n not in xw:
-                xw[n] = sb.tile([P, WIDTHS[n] // P, D], BF16, name="xw", bufs=8)
-            nc.vector.tensor_copy(
-                out=xw[n][:, 1, :VECTOR_COLUMNS], in_=xb[n][:, 1, :VECTOR_COLUMNS].bitcast(FP8)
-            )
+                nc.scalar.copy(out=xw[n][:, s], in_=codes)
 
         def x_transpose(n, g):
             if not valid(n):
                 return
-            t = psum.tile([P, 2, WIDTHS[n]], F32, name="xt", bufs=3)
-            for s in slabs(n):
+            xt[n, g] = psum.tile([P, 2, STEP], F32, name="xt", bufs=3)
+            for s in range(SLABS):
                 words = xw[n][:, s].bitcast(F32)
                 for u in range(2):
-                    nc.tensor.transpose(t[:, u, cols(s)], words[:, 256 * g + u : 256 * (g + 1) : 2], ident[:])
-            xt[n, g] = t
+                    nc.tensor.transpose(
+                        xt[n, g][:, u, cols(s)], words[:, 256 * g + u : 256 * (g + 1) : 2], ident[:]
+                    )
 
-        def new_xg(n):
+        def packed_x(n):
             if n not in xg:
-                xg[n] = sb.tile([P, G, WIDTHS[n], 4], BF16, align_bytes=64, name="xg")
+                xg[n] = sb.tile([P, GROUPS, STEP, PACK], BF16, align_bytes=64, name="xg")
+            return xg[n]
 
         def x_copy(n):
             if not valid(n) or not pool_tokens(n):
                 return
-            first = WIDTHS[n] - pool_tokens(n)
-            t = sb.tile([P, pool_tokens(n), 4], BF16, align_bytes=64, name="xi")
+            first = STEP - pool_tokens(n)
+            xi[n] = sb.tile([P, pool_tokens(n), PACK], BF16, align_bytes=64, name="xi")
             nc.scalar.copy(
-                out=t[:].rearrange("p n t -> p (n t)").bitcast(F32).rearrange("p (n u) -> p n u", u=2),
+                out=xi[n][:].rearrange("p n t -> p (n t)").bitcast(F32).rearrange("p (n u) -> p n u", u=2),
                 in_=xt[n, 1][:, :, first:].rearrange("p u n -> p n u"),
             )
-            xi[n] = t
 
         def x_scale_pool(n):
             if not valid(n) or not pool_tokens(n):
                 return
-            new_xg(n)
-            count = pool_tokens(n)
-            nc.gpsimd.tensor_tensor(
-                out=xg[n][:, 1, WIDTHS[n] - count :],
-                in0=xi[n][:],
-                in1=xs[:, 1].unsqueeze(1).to_broadcast([P, count, 4]),
-                op=ALU.mult,
-            )
+            packed = packed_x(n)
+            first = STEP - pool_tokens(n)
+            half = pool_tokens(n) // 2
+            for h in range(2):
+                nc.gpsimd.tensor_tensor(
+                    out=packed[:, 1, first + half * h : first + half * (h + 1)],
+                    in0=xi[n][:, half * h : half * (h + 1)],
+                    in1=xs[:, 1].unsqueeze(1).to_broadcast([P, half, PACK]),
+                    op=ALU.mult,
+                )
 
         def x_scale_vector(n, g):
             if not valid(n):
                 return
-            new_xg(n)
-            count = WIDTHS[n] - (pool_tokens(n) if g == 1 else 0)
+            packed = packed_x(n)
+            count = STEP - (pool_tokens(n) if g == 1 else 0)
             values = xt[n, g][:].rearrange("p u n -> p (u n)").bitcast(BF16)
             nc.vector.tensor_tensor(
-                out=xg[n][:, g, :count].rearrange("p n (u e) -> p n u e", u=2),
+                out=packed[:, g, :count].rearrange("p n (u e) -> p n u e", u=2),
                 in0=values.rearrange("p (u n e) -> p n u e", u=2, e=2)[:, :count],
                 in1=xs[:, g].rearrange("p (u e) -> p u e", u=2).unsqueeze(1).to_broadcast([P, count, 2, 2]),
                 op=ALU.mult,
@@ -180,8 +213,8 @@ def tile_rankwisemoloradenserouter_t_kernel(tc, x_bytes, x_scale, w0, wr, br, a,
         def x_quantize(n):
             if not valid(n):
                 return
-            xc[n] = sb.tile([P, G, WIDTHS[n]], U32, align_bytes=64, name="xc", bufs=10)
-            xsc[n] = sb.tile([P, G, WIDTHS[n]], U8, align_bytes=64, name="xsc", bufs=10)
+            xc[n] = sb.tile([P, GROUPS, STEP], U32, align_bytes=64, name="xc")
+            xsc[n] = sb.tile([P, GROUPS, STEP], U8, align_bytes=64, name="xsc")
             quantize(
                 xc[n][:].rearrange("p g n -> p (g n)"),
                 xsc[n][:].rearrange("p g n -> p (g n)"),
@@ -192,38 +225,36 @@ def tile_rankwisemoloradenserouter_t_kernel(tc, x_bytes, x_scale, w0, wr, br, a,
             if not valid(n):
                 return
             sm[n] = psum.tile([P, 2, STEP], F32, name="sm")
-            for g in range(G):
+            for g in range(GROUPS):
                 nc.tensor.matmul_mx(
-                    out=sm[n][:, 0, : WIDTHS[n]],
+                    out=sm[n][:, 0],
                     lhsT=wr_c[:, g].bitcast(FP8X4),
                     lhsT_scale=wr_s[:, g],
                     rhs=xc[n][:, g].bitcast(FP8X4),
                     rhs_scale=xsc[n][:, g],
                     start=(g == 0),
-                    stop=(g == G - 1),
+                    stop=(g == GROUPS - 1),
                 )
 
         def bias(n):
             if not valid(n):
                 return
-            lT_sb[n] = sb.tile([P, WIDTHS[n]], F32, name="lT_sb")
-            nc.scalar.activation(
-                out=lT_sb[n][:], in_=sm[n][:, 0, : WIDTHS[n]], func=ACT.Identity, bias=br_col[:], scale=1.0
-            )
+            lT[n] = sb.tile([P, STEP], F32, name="lT")
+            nc.scalar.activation(out=lT[n][:], in_=sm[n][:, 0], func=ACT.Identity, bias=br_col[:], scale=1.0)
 
         def l_transpose(n):
             if not valid(n):
                 return
-            for s in slabs(n):
-                nc.tensor.transpose(sm[n][:, 1, cols(s)], lT_sb[n][:, cols(s)], ident[:])
+            for s in range(SLABS):
+                nc.tensor.transpose(sm[n][:, 1, cols(s)], lT[n][:, cols(s)], ident[:])
 
         def rowmax(n):
             if not valid(n):
                 return
-            negmax[n] = sb.tile([P, WIDTHS[n] // P], F32, name="negmax")
+            negmax[n] = sb.tile([P, SLABS], F32, name="negmax")
             nc.vector.tensor_reduce(
                 out=negmax[n][:],
-                in_=sm[n][:, 1, : WIDTHS[n]].rearrange("p (s e) -> p s e", e=E),
+                in_=sm[n][:, 1].rearrange("p (s e) -> p s e", e=E),
                 axis=AX.X,
                 op=ALU.max,
                 negate=True,
@@ -232,9 +263,9 @@ def tile_rankwisemoloradenserouter_t_kernel(tc, x_bytes, x_scale, w0, wr, br, a,
         def expo(n):
             if not valid(n):
                 return
-            ex[n] = sb.tile([P, WIDTHS[n] // P, E], F32, name="ex")
-            esum[n] = sb.tile([P, WIDTHS[n] // P], F32, name="esum")
-            for s in slabs(n):
+            ex[n] = sb.tile([P, SLABS, E], F32, name="ex")
+            esum[n] = sb.tile([P, SLABS], F32, name="esum")
+            for s in range(SLABS):
                 nc.scalar.activation(
                     out=ex[n][:, s],
                     in_=sm[n][:, 1, cols(s)],
@@ -247,14 +278,14 @@ def tile_rankwisemoloradenserouter_t_kernel(tc, x_bytes, x_scale, w0, wr, br, a,
         def recip(n):
             if not valid(n):
                 return
-            rsum[n] = sb.tile([P, WIDTHS[n] // P], F32, name="rsum")
+            rsum[n] = sb.tile([P, SLABS], F32, name="rsum")
             nc.vector.reciprocal(out=rsum[n][:], in_=esum[n][:])
 
         def normalise(n):
             if not valid(n):
                 return
-            gn[n] = sb.tile([P, WIDTHS[n] // P, E], F32, name="gn")
-            for s in slabs(n):
+            gn[n] = sb.tile([P, SLABS, E], F32, name="gn")
+            for s in range(SLABS):
                 nc.gpsimd.tensor_scalar(
                     gn[n][:, s], ex[n][:, s], rsum[n][:, s : s + 1], float(E), op0=ALU.mult, op1=ALU.mult
                 )
@@ -262,57 +293,56 @@ def tile_rankwisemoloradenserouter_t_kernel(tc, x_bytes, x_scale, w0, wr, br, a,
         def g_transpose(n):
             if not valid(n):
                 return
-            for s in slabs(n):
+            for s in range(SLABS):
                 nc.tensor.transpose(sm[n][:, 0, cols(s)], gn[n][:, s], ident[:])
 
         def g_copy(n):
             if not valid(n):
                 return
-            g_sb[n] = sb.tile([P, WIDTHS[n]], F32, name="g_sb")
-            nc.scalar.copy(out=g_sb[n][:], in_=sm[n][:, 0, : WIDTHS[n]])
+            gT[n] = sb.tile([P, STEP], F32, name="gT")
+            nc.scalar.copy(out=gT[n][:], in_=sm[n][:, 0])
 
         def down(n, s):
-            if not valid(n, s):
+            if not valid(n):
                 return
-            t = psum.tile([P, 4, P], F32, name="ub")
-            for c in range(4):
-                for g in range(G):
+            ub[n, s] = psum.tile([P, PACK, P], F32, name="ub")
+            for c in range(PACK):
+                for g in range(GROUPS):
                     nc.tensor.matmul_mx(
-                        out=t[:, c],
+                        out=ub[n, s][:, c],
                         lhsT=a_c[:, g, cols(c)].bitcast(FP8X4),
                         lhsT_scale=a_s[:, g, cols(c)],
                         rhs=xc[n][:, g, cols(s)].bitcast(FP8X4),
                         rhs_scale=xsc[n][:, g, cols(s)],
                         start=(g == 0),
-                        stop=(g == G - 1),
+                        stop=(g == GROUPS - 1),
                     )
-            ub[n, s] = t
 
         def gate(n, s):
-            if not valid(n, s):
+            if not valid(n):
                 return
             if n not in zg:
-                zg[n] = sb.tile([P, WIDTHS[n], 4], BF16, align_bytes=64, name="zg")
+                zg[n] = sb.tile([P, STEP, PACK], BF16, align_bytes=64, name="zg")
             nc.vector.tensor_tensor(
                 out=zg[n][:, cols(s)],
                 in0=ub[n, s][:].rearrange("p c n -> p n c"),
-                in1=g_sb[n][:, cols(s)].unsqueeze(2).to_broadcast([P, P, 4]),
+                in1=gT[n][:, cols(s)].unsqueeze(2).to_broadcast([P, P, PACK]),
                 op=ALU.mult,
             )
 
         def z_quantize(n):
             if not valid(n):
                 return
-            zc[n] = sb.tile([P, WIDTHS[n]], U32, align_bytes=64, name="zc")
-            zs[n] = sb.tile([P, WIDTHS[n]], U8, align_bytes=64, name="zs")
+            zc[n] = sb.tile([P, STEP], U32, align_bytes=64, name="zc")
+            zs[n] = sb.tile([P, STEP], U8, align_bytes=64, name="zs")
             quantize(zc[n][:], zs[n][:], zg[n][:].rearrange("p n t -> p (n t)"))
 
         def combine(n):
             if not valid(n):
                 return
-            yb[n] = psum.tile([P, WIDTHS[n] // P, F], F32, name="yb", bufs=1)
-            for s in slabs(n):
-                for g in range(G):
+            yb[n] = psum.tile([P, SLABS, F], F32, name="yb", bufs=1)
+            for s in range(SLABS):
+                for g in range(GROUPS):
                     nc.tensor.matmul_mx(
                         out=yb[n][:, s],
                         lhsT=xc[n][:, g, cols(s)].bitcast(FP8X4),
@@ -335,95 +365,51 @@ def tile_rankwisemoloradenserouter_t_kernel(tc, x_bytes, x_scale, w0, wr, br, a,
         def store(n):
             if not valid(n):
                 return
-            y = sb.tile([P, WIDTHS[n] // P, F], F32, name="y")
+            y = sb.tile([P, SLABS, F], F32, name="y")
             nc.scalar.copy(out=y[:], in_=yb[n][:])
             nc.sync.dma_start(out=rows(out, n), in_=y[:])
 
-        def wr_group():
-            nc.vector.tensor_copy(out=wr_g[:], in_=wr_raw[:].rearrange("p g j n -> p g n j"))
-
-        def wr_quantize():
-            quantize(
-                wr_c[:].rearrange("p g n -> p (g n)"),
-                wr_s[:].rearrange("p g n -> p (g n)"),
-                wr_g[:].rearrange("p g n t -> p (g n t)"),
-            )
-
-        def a_group(g):
-            dst = a_g[:, g].rearrange("p (t m) j -> p t m j", t=4)
-            src = a_raw[:, g].rearrange("p j (m t) -> p t m j", t=4)
-            if g == 0:
-                for c in range(4):
-                    pool_copy(dst[:, c], src[:, c])
-            else:
-                nc.vector.tensor_copy(out=dst, in_=src)
-
-        def a_quantize(g):
-            quantize(a_c[:, g], a_s[:, g], a_g[:, g].rearrange("p n t -> p (n t)"))
-
-        def w0_group():
-            for g in range(G):
-                for h in range(2):
-                    pool_copy(w0_g[:, g, cols(h)], w0_raw[:, g, :, cols(h)].rearrange("p j n -> p n j"))
-
-        def w0_quantize():
-            quantize(
-                w0_c[:].rearrange("p g n -> p (g n)"),
-                w0_s[:].rearrange("p g n -> p (g n)"),
-                w0_g[:].rearrange("p g n t -> p (g n t)"),
-            )
-
-        def b_group():
-            for h in range(2):
-                pool_copy(b_g[:, cols(h)], b_raw[:, :, cols(h)].rearrange("p j n -> p n j"))
-
-        def b_quantize():
-            quantize(b_c[:], b_s[:], b_g[:].rearrange("p n t -> p (n t)"))
-
-        for n in range(-4, N_STEPS + 3):
-            gate(n - 2, 0)
+        wr_pack()
+        a_pack(0)
+        for n in range(-5, N_STEPS + 3):
+            if n == 3:
+                w0_pack()
+            g_transpose(n - 2)
+            if n == 2:
+                a_quantize(0)
+            g_copy(n - 2)
+            rowmax(n - 1)
+            down(n - 2, 1)
+            x_transpose(n + 3, 1)
+            x_quantize(n)
+            down(n - 2, 0)
+            z_quantize(n - 3)
+            if n == 3:
+                w0_quantize()
             expo(n - 1)
             recip(n - 1)
-            gate(n - 2, 1)
-            widen_vector(n + 3)
-            logits(n)
-            down(n - 1, 0)
-            if n == -1:
-                wr_quantize()
-            if n == 2:
-                w0_group()
-            x_transpose(n + 2, 1)
-            x_scale_vector(n + 1, 1)
-            if n == 1:
-                b_group()
-            normalise(n - 1)
-            if n == 0:
-                a_group(0)
-            x_scale_vector(n + 1, 0)
-            widen(n + 4, 0)
-            bias(n)
-            g_transpose(n - 1)
-            if n == 0:
-                a_quantize(0)
-            if n == 0:
-                a_quantize(1)
-            widen(n + 3, 1)
-            l_transpose(n)
-            if n == -3:
-                wr_group()
             if n == 2:
                 b_quantize()
-            x_transpose(n + 2, 0)
-            store(n - 3)
-            z_quantize(n - 2)
-            g_copy(n - 1)
-            down(n - 1, 1)
-            rowmax(n)
-            if n == -1:
-                a_group(1)
-            if n == 2:
-                w0_quantize()
+            gate(n - 2, 1)
+            if n == -2:
+                wr_quantize()
             x_scale_pool(n + 1)
-            x_copy(n + 2)
-            x_quantize(n + 1)
-            combine(n - 2)
+            logits(n)
+            x_scale_vector(n + 1, 0)
+            combine(n - 3)
+            widen(n + 5, 0)
+            bias(n)
+            x_copy(n + 3)
+            x_scale_vector(n + 3, 1)
+            if n == -1:
+                a_pack(1)
+            if n == 1:
+                b_pack()
+            widen(n + 5, 1)
+            x_transpose(n + 2, 0)
+            l_transpose(n)
+            gate(n - 2, 0)
+            normalise(n - 1)
+            store(n - 3)
+            if n == 0:
+                a_quantize(1)

from contextlib import ExitStack

import concourse.mybir as mybir
from concourse.masks import make_identity

T, D, F, E, R = 4096, 1024, 256, 128, 512
P = 128
PACK = 4
GROUPS = D // (P * PACK)
STEP = 256
N_STEPS = T // STEP
SLABS = STEP // P
POOL_TOKENS = 128
WIDENED_ON_VECTOR = ((0, 1), (1, 1))

FLOPS = 2 * T * D * (F + E + R) + 2 * T * R * F

F32 = mybir.dt.float32
BF16 = mybir.dt.bfloat16
U32 = mybir.dt.uint32
U8 = mybir.dt.uint8
FP8 = mybir.dt.float8_e4m3fn
FP8X4 = mybir.dt.float8_e4m3fn_x4
ACT = mybir.ActivationFunctionType
ALU = mybir.AluOpType
AX = mybir.AxisListType


def tile_rankwisemoloradenserouter_t_kernel(tc, x_bytes, x_scale, w0, wr, br, a, b, out):
    nc = tc.nc
    with ExitStack() as ctx:
        keep = ctx.enter_context(tc.tile_pool(name="keep", bufs=1))
        bytes_pool = ctx.enter_context(tc.tile_pool(name="xbytes", bufs=N_STEPS))
        sb = ctx.enter_context(tc.tile_pool(name="sb", bufs=5))
        psum = ctx.enter_context(tc.psum_pool(name="psum", bufs=2))
        ctx.enter_context(tc.manual_schedule())

        def rows(ap, n):
            return ap[n * STEP : (n + 1) * STEP, :].rearrange("(p s) k -> p s k", s=SLABS)

        def cols(i):
            return slice(P * i, P * (i + 1))

        xb = {}

        def load_x(n):
            xb[n] = bytes_pool.tile([P, SLABS, D], U8, name="xb")
            nc.sync.dma_start(out=xb[n][:], in_=rows(x_bytes, n))

        wr_raw = keep.tile([P, GROUPS, PACK, E], BF16, name="wr_raw")
        a_raw = keep.tile([P, GROUPS, PACK, R], BF16, name="a_raw")
        w0_raw = keep.tile([P, GROUPS, PACK, F], BF16, name="w0_raw")
        b_raw = keep.tile([P, PACK, F], BF16, name="b_raw")
        xs = keep.tile([P, GROUPS, PACK], F32, name="xs")
        br_col = keep.tile([P, 1], BF16, name="br_col")

        load_x(0)
        nc.sync.dma_start(out=wr_raw[:], in_=wr.rearrange("(g p j) n -> p g j n", g=GROUPS, j=PACK))
        load_x(1)
        nc.sync.dma_start(out=xs[:], in_=x_scale.rearrange("o (g p t) -> p (o g) t", g=GROUPS, t=PACK))
        with nc.allow_non_contiguous_dma(reason="one bias value to a partition"):
            nc.sync.dma_start(out=br_col[:], in_=br.rearrange("(p o) -> p o", o=1))
        load_x(2)
        for g in range(GROUPS):
            a_rows = a[P * PACK * g : P * PACK * (g + 1), :]
            nc.sync.dma_start(out=a_raw[:, g], in_=a_rows.rearrange("(p j) n -> p j n", j=PACK))
        load_x(3)
        nc.sync.dma_start(out=w0_raw[:], in_=w0.rearrange("(g p j) n -> p g j n", g=GROUPS, j=PACK))
        nc.sync.dma_start(out=b_raw[:], in_=b.rearrange("(p j) n -> p j n", j=PACK))
        for n in range(4, N_STEPS):
            load_x(n)

        warm = keep.tile([P, 1], F32, name="warm")
        nc.vector.memset(warm[:], 0.0)
        nc.scalar.activation(out=warm[:], in_=warm[:], func=ACT.Exp)
        ident = keep.tile([P, P], F32, name="ident")
        make_identity(nc, ident[:])

        wr_g = keep.tile([P, GROUPS, E, PACK], BF16, align_bytes=64, name="wr_g")
        a_g = keep.tile([P, GROUPS, R, PACK], BF16, align_bytes=64, name="a_g")
        w0_g = keep.tile([P, GROUPS, F, PACK], BF16, align_bytes=64, name="w0_g")
        b_g = keep.tile([P, F, PACK], BF16, align_bytes=64, name="b_g")
        wr_c = keep.tile([P, GROUPS, E], U32, align_bytes=64, name="wr_c")
        wr_s = keep.tile([P, GROUPS, E], U8, align_bytes=64, name="wr_s")
        a_c = keep.tile([P, GROUPS, R], U32, align_bytes=64, name="a_c")
        a_s = keep.tile([P, GROUPS, R], U8, align_bytes=64, name="a_s")
        w0_c = keep.tile([P, GROUPS, F], U32, align_bytes=64, name="w0_c")
        w0_s = keep.tile([P, GROUPS, F], U8, align_bytes=64, name="w0_s")
        b_c = keep.tile([P, F], U32, align_bytes=64, name="b_c")
        b_s = keep.tile([P, F], U8, align_bytes=64, name="b_s")

        def quantize(codes, scales, packed):
            nc.vector.quantize_mx(out=codes.bitcast(FP8X4), scales=scales, in_=packed)

        def pool_copy(dst, src):
            nc.gpsimd.tensor_scalar(dst, src, 1.0, 0.0, op0=ALU.mult, op1=ALU.add)

        def wr_pack():
            nc.vector.tensor_copy(out=wr_g[:], in_=wr_raw[:].rearrange("p g j n -> p g n j"))

        def wr_quantize():
            quantize(
                wr_c[:].rearrange("p g n -> p (g n)"),
                wr_s[:].rearrange("p g n -> p (g n)"),
                wr_g[:].rearrange("p g n t -> p (g n t)"),
            )

        def a_pack(g):
            dst = a_g[:, g].rearrange("p (c m) j -> p c m j", c=PACK)
            src = a_raw[:, g].rearrange("p j (m c) -> p c m j", c=PACK)
            if g == 0:
                for c in range(PACK):
                    pool_copy(dst[:, c], src[:, c])
            else:
                nc.vector.tensor_copy(out=dst, in_=src)

        def a_quantize(g):
            quantize(a_c[:, g], a_s[:, g], a_g[:, g].rearrange("p n t -> p (n t)"))

        def w0_pack():
            for g in range(GROUPS):
                for h in range(F // P):
                    pool_copy(w0_g[:, g, cols(h)], w0_raw[:, g, :, cols(h)].rearrange("p j n -> p n j"))

        def w0_quantize():
            quantize(
                w0_c[:].rearrange("p g n -> p (g n)"),
                w0_s[:].rearrange("p g n -> p (g n)"),
                w0_g[:].rearrange("p g n t -> p (g n t)"),
            )

        def b_pack():
            for h in range(F // P):
                pool_copy(b_g[:, cols(h)], b_raw[:, :, cols(h)].rearrange("p j n -> p n j"))

        def b_quantize():
            quantize(b_c[:], b_s[:], b_g[:].rearrange("p n t -> p (n t)"))

        xw, xt, xi, xg, xc, xsc = {}, {}, {}, {}, {}, {}
        sm, lT, negmax, ex, esum, rsum, gn, gT = {}, {}, {}, {}, {}, {}, {}, {}
        ub, zg, zc, zs, yb = {}, {}, {}, {}, {}

        def valid(n):
            return 0 <= n < N_STEPS

        def pool_tokens(n):
            return POOL_TOKENS if n > 0 else 0

        def widen(n, s):
            if not valid(n):
                return
            if n not in xw:
                xw[n] = sb.tile([P, SLABS, D], BF16, name="xw")
            codes = xb[n][:, s].bitcast(FP8)
            if (n, s) in WIDENED_ON_VECTOR:
                nc.vector.tensor_copy(out=xw[n][:, s], in_=codes)
            else:
                nc.scalar.copy(out=xw[n][:, s], in_=codes)

        def x_transpose(n, g):
            if not valid(n):
                return
            xt[n, g] = psum.tile([P, 2, STEP], F32, name="xt", bufs=3)
            for s in range(SLABS):
                words = xw[n][:, s].bitcast(F32)
                for u in range(2):
                    nc.tensor.transpose(
                        xt[n, g][:, u, cols(s)], words[:, 256 * g + u : 256 * (g + 1) : 2], ident[:]
                    )

        def packed_x(n):
            if n not in xg:
                xg[n] = sb.tile([P, GROUPS, STEP, PACK], BF16, align_bytes=64, name="xg")
            return xg[n]

        def x_copy(n):
            if not valid(n) or not pool_tokens(n):
                return
            first = STEP - pool_tokens(n)
            xi[n] = sb.tile([P, pool_tokens(n), PACK], BF16, align_bytes=64, name="xi")
            nc.scalar.copy(
                out=xi[n][:].rearrange("p n t -> p (n t)").bitcast(F32).rearrange("p (n u) -> p n u", u=2),
                in_=xt[n, 1][:, :, first:].rearrange("p u n -> p n u"),
            )

        def x_scale_pool(n):
            if not valid(n) or not pool_tokens(n):
                return
            packed = packed_x(n)
            first = STEP - pool_tokens(n)
            half = pool_tokens(n) // 2
            for h in range(2):
                nc.gpsimd.tensor_tensor(
                    out=packed[:, 1, first + half * h : first + half * (h + 1)],
                    in0=xi[n][:, half * h : half * (h + 1)],
                    in1=xs[:, 1].unsqueeze(1).to_broadcast([P, half, PACK]),
                    op=ALU.mult,
                )

        def x_scale_vector(n, g):
            if not valid(n):
                return
            packed = packed_x(n)
            count = STEP - (pool_tokens(n) if g == 1 else 0)
            values = xt[n, g][:].rearrange("p u n -> p (u n)").bitcast(BF16)
            nc.vector.tensor_tensor(
                out=packed[:, g, :count].rearrange("p n (u e) -> p n u e", u=2),
                in0=values.rearrange("p (u n e) -> p n u e", u=2, e=2)[:, :count],
                in1=xs[:, g].rearrange("p (u e) -> p u e", u=2).unsqueeze(1).to_broadcast([P, count, 2, 2]),
                op=ALU.mult,
            )

        def x_quantize(n):
            if not valid(n):
                return
            xc[n] = sb.tile([P, GROUPS, STEP], U32, align_bytes=64, name="xc")
            xsc[n] = sb.tile([P, GROUPS, STEP], U8, align_bytes=64, name="xsc")
            quantize(
                xc[n][:].rearrange("p g n -> p (g n)"),
                xsc[n][:].rearrange("p g n -> p (g n)"),
                xg[n][:].rearrange("p g n t -> p (g n t)"),
            )

        def logits(n):
            if not valid(n):
                return
            sm[n] = psum.tile([P, 2, STEP], F32, name="sm")
            for g in range(GROUPS):
                nc.tensor.matmul_mx(
                    out=sm[n][:, 0],
                    lhsT=wr_c[:, g].bitcast(FP8X4),
                    lhsT_scale=wr_s[:, g],
                    rhs=xc[n][:, g].bitcast(FP8X4),
                    rhs_scale=xsc[n][:, g],
                    start=(g == 0),
                    stop=(g == GROUPS - 1),
                )

        def bias(n):
            if not valid(n):
                return
            lT[n] = sb.tile([P, STEP], F32, name="lT")
            nc.scalar.activation(out=lT[n][:], in_=sm[n][:, 0], func=ACT.Identity, bias=br_col[:], scale=1.0)

        def l_transpose(n):
            if not valid(n):
                return
            for s in range(SLABS):
                nc.tensor.transpose(sm[n][:, 1, cols(s)], lT[n][:, cols(s)], ident[:])

        def rowmax(n):
            if not valid(n):
                return
            negmax[n] = sb.tile([P, SLABS], F32, name="negmax")
            nc.vector.tensor_reduce(
                out=negmax[n][:],
                in_=sm[n][:, 1].rearrange("p (s e) -> p s e", e=E),
                axis=AX.X,
                op=ALU.max,
                negate=True,
            )

        def expo(n):
            if not valid(n):
                return
            ex[n] = sb.tile([P, SLABS, E], F32, name="ex")
            esum[n] = sb.tile([P, SLABS], F32, name="esum")
            for s in range(SLABS):
                nc.scalar.activation(
                    out=ex[n][:, s],
                    in_=sm[n][:, 1, cols(s)],
                    func=ACT.Exp,
                    bias=negmax[n][:, s : s + 1],
                    scale=1.0,
                    accum_out=esum[n][:, s : s + 1],
                )

        def recip(n):
            if not valid(n):
                return
            rsum[n] = sb.tile([P, SLABS], F32, name="rsum")
            nc.vector.reciprocal(out=rsum[n][:], in_=esum[n][:])

        def normalise(n):
            if not valid(n):
                return
            gn[n] = sb.tile([P, SLABS, E], F32, name="gn")
            for s in range(SLABS):
                nc.gpsimd.tensor_scalar(
                    gn[n][:, s], ex[n][:, s], rsum[n][:, s : s + 1], float(E), op0=ALU.mult, op1=ALU.mult
                )

        def g_transpose(n):
            if not valid(n):
                return
            for s in range(SLABS):
                nc.tensor.transpose(sm[n][:, 0, cols(s)], gn[n][:, s], ident[:])

        def g_copy(n):
            if not valid(n):
                return
            gT[n] = sb.tile([P, STEP], F32, name="gT")
            nc.scalar.copy(out=gT[n][:], in_=sm[n][:, 0])

        def down(n, s):
            if not valid(n):
                return
            ub[n, s] = psum.tile([P, PACK, P], F32, name="ub")
            for c in range(PACK):
                for g in range(GROUPS):
                    nc.tensor.matmul_mx(
                        out=ub[n, s][:, c],
                        lhsT=a_c[:, g, cols(c)].bitcast(FP8X4),
                        lhsT_scale=a_s[:, g, cols(c)],
                        rhs=xc[n][:, g, cols(s)].bitcast(FP8X4),
                        rhs_scale=xsc[n][:, g, cols(s)],
                        start=(g == 0),
                        stop=(g == GROUPS - 1),
                    )

        def gate(n, s):
            if not valid(n):
                return
            if n not in zg:
                zg[n] = sb.tile([P, STEP, PACK], BF16, align_bytes=64, name="zg")
            nc.vector.tensor_tensor(
                out=zg[n][:, cols(s)],
                in0=ub[n, s][:].rearrange("p c n -> p n c"),
                in1=gT[n][:, cols(s)].unsqueeze(2).to_broadcast([P, P, PACK]),
                op=ALU.mult,
            )

        def z_quantize(n):
            if not valid(n):
                return
            zc[n] = sb.tile([P, STEP], U32, align_bytes=64, name="zc")
            zs[n] = sb.tile([P, STEP], U8, align_bytes=64, name="zs")
            quantize(zc[n][:], zs[n][:], zg[n][:].rearrange("p n t -> p (n t)"))

        def combine(n):
            if not valid(n):
                return
            yb[n] = psum.tile([P, SLABS, F], F32, name="yb", bufs=1)
            for s in range(SLABS):
                for g in range(GROUPS):
                    nc.tensor.matmul_mx(
                        out=yb[n][:, s],
                        lhsT=xc[n][:, g, cols(s)].bitcast(FP8X4),
                        lhsT_scale=xsc[n][:, g, cols(s)],
                        rhs=w0_c[:, g].bitcast(FP8X4),
                        rhs_scale=w0_s[:, g],
                        start=(g == 0),
                        stop=False,
                    )
                nc.tensor.matmul_mx(
                    out=yb[n][:, s],
                    lhsT=zc[n][:, cols(s)].bitcast(FP8X4),
                    lhsT_scale=zs[n][:, cols(s)],
                    rhs=b_c[:].bitcast(FP8X4),
                    rhs_scale=b_s[:],
                    start=False,
                    stop=True,
                )

        def store(n):
            if not valid(n):
                return
            y = sb.tile([P, SLABS, F], F32, name="y")
            nc.scalar.copy(out=y[:], in_=yb[n][:])
            nc.sync.dma_start(out=rows(out, n), in_=y[:])

        wr_pack()
        a_pack(0)
        for n in range(-5, N_STEPS + 3):
            if n == 3:
                w0_pack()
            g_transpose(n - 2)
            if n == 2:
                a_quantize(0)
            g_copy(n - 2)
            rowmax(n - 1)
            down(n - 2, 1)
            x_transpose(n + 3, 1)
            x_quantize(n)
            down(n - 2, 0)
            z_quantize(n - 3)
            if n == 3:
                w0_quantize()
            expo(n - 1)
            recip(n - 1)
            if n == 2:
                b_quantize()
            gate(n - 2, 1)
            if n == -2:
                wr_quantize()
            x_scale_pool(n + 1)
            logits(n)
            x_scale_vector(n + 1, 0)
            combine(n - 3)
            widen(n + 5, 0)
            bias(n)
            x_copy(n + 3)
            x_scale_vector(n + 3, 1)
            if n == -1:
                a_pack(1)
            if n == 1:
                b_pack()
            widen(n + 5, 1)
            x_transpose(n + 2, 0)
            l_transpose(n)
            gate(n - 2, 0)
            normalise(n - 1)
            store(n - 3)
            if n == 0:
                a_quantize(1)
